import numpy as np
import ml_dtypes


def mxq(x, axis, fmt="e4m3"):
    dtype, down = {"e4m3": (ml_dtypes.float8_e4m3fn, 7), "e5m2": (ml_dtypes.float8_e5m2, 14)}[fmt]
    v = np.moveaxis(np.asarray(x, np.float32).astype(ml_dtypes.bfloat16).astype(np.float64), axis, -1)
    blocks = v.reshape(v.shape[:-1] + (-1, 32))
    amax = np.abs(blocks).max(-1, keepdims=True)
    byte = np.maximum(np.where(amax > 0, np.frexp(amax)[1] - 1 + 127, 0) - down, 1)
    scale = np.exp2(byte - 127.0)
    codes = (blocks / scale).astype(np.float32).astype(dtype).astype(np.float64)
    return np.moveaxis((codes * scale).reshape(v.shape), -1, axis)


WIDE = False


def mx_kscale(k):
    if not WIDE:
        return np.ones(k)
    levels = np.array([10, -10, 5, -5, 0])
    if k % 512:
        return np.exp2(np.random.permutation(np.resize(levels, k // 32))).repeat(32)
    a = np.empty((k // 512, 16))
    for p in range(k // 512):
        a[p, :8] = np.random.permutation(np.resize(levels, 8))
        for g in range(8):
            far = levels[np.abs(levels - a[p, g]) >= 10]
            a[p, g + 8] = far[np.random.randint(len(far))]
    return np.exp2(a.ravel()).repeat(32)


def f64(x):
    return np.asarray(x).astype(np.float64)


def striped(idx):
    return np.tile(np.asarray(idx).reshape(-1, 16).T, (8, 1)).astype(np.uint16)


def unstriped(offs):
    return offs[:16].T.reshape(-1).astype(np.int64)


E2M1 = np.array([0.0, 0.5, 1.0, 1.5, 2.0, 3.0, 4.0, 6.0, -0.0, -0.5, -1.0, -1.5, -2.0, -3.0, -4.0, -6.0])


def pack_weight(w, fmt):
    k, n = w.shape
    w = f64(np.asarray(w, np.float32).astype(ml_dtypes.bfloat16)).reshape(k // 32, 32, n)
    amax = np.abs(w).max(1)
    if fmt == "e4m3":
        byte = np.frexp(amax)[1] - 1 + 127 - 7
    else:
        mant, ex = np.frexp(amax / 6.0)
        byte = np.where(mant > 0.5, ex, ex - 1) + 127
    byte = np.clip(np.where(amax > 0, byte, 1), 1, 254)
    scaled = (w * np.exp2(127.0 - byte)[:, None, :]).reshape(k, n).astype(np.float32)
    by_word = np.ascontiguousarray(scaled.reshape(k // 512, 128, 4, n).transpose(0, 1, 3, 2))
    if fmt == "e4m3":
        words = by_word.astype(ml_dtypes.float8_e4m3fn).view(np.uint8)
    else:
        c = by_word.astype(ml_dtypes.float4_e2m1fn).view(np.uint8) & 0xF
        words = (c[..., 0::2] | (c[..., 1::2] << 4)).reshape(k // 512, 128, 2 * n)
    return np.ascontiguousarray(words), np.ascontiguousarray(byte.astype(np.uint8).reshape(k // 512, 16, n))


def unpack_weight(words, scales, fmt):
    g, _, n = scales.shape
    words = np.ascontiguousarray(words).reshape(g, 128, n, -1)
    if fmt == "e4m3":
        vals = words.view(ml_dtypes.float8_e4m3fn).astype(np.float64)
    else:
        nib = np.empty((g, 128, n, 4), np.uint8)
        nib[..., 0::2] = words & 0xF
        nib[..., 1::2] = words >> 4
        vals = E2M1[nib]
    vals = vals * np.repeat(np.exp2(scales.astype(np.float64) - 127.0), 8, axis=1)[..., None]
    return vals.transpose(0, 1, 3, 2).reshape(g * 512, n)


K, T, J, N = 512, 2048, 512, 256


def setup_inputs():
    n = np.random.standard_normal
    idx = np.random.permutation(T)[:J]
    idx2 = np.random.permutation(T)[:J]
    fk = mx_kscale(K)
    xqp = pack_weight(n((K, T)) / fk[:, None], "e2m1")
    wbp = pack_weight(n((K, N)) * 1 / np.sqrt(K) * fk[:, None], "e4m3")
    wmp = pack_weight(n((K, N)) * 1 / np.sqrt(K) * fk[:, None], "e2m1")
    return {
        "xq_words": xqp[0],
        "xq_scales": xqp[1],
        "wb_words": wbp[0],
        "wb_scales": wbp[1],
        "xf": (n((K, T)) / fk[:, None]).astype(np.float32),
        "sh": (np.random.uniform(0.3, 0.7, (1, J))).astype(np.float32),
        "wm_words": wmp[0],
        "wm_scales": wmp[1],
        "offs": striped(idx),
        "offs2": striped(idx2),
    }


def reference(xq_words, xq_scales, wb_words, wb_scales, xf, sh, wm_words, wm_scales, offs, offs2):
    idx = unstriped(offs)
    idx2 = unstriped(offs2)
    xqu = unpack_weight(xq_words, xq_scales, "e2m1")
    wbu = unpack_weight(wb_words, wb_scales, "e4m3")
    wmu = unpack_weight(wm_words, wm_scales, "e2m1")
    z = wbu.T @ xqu
    xm = f64(xf)[:, idx2] + f64(sh) * (f64(xf)[:, idx] - f64(xf)[:, idx2])
    xmq = mxq(xm, 0, "e4m3")
    p = wmu.T @ xmq
    pa = np.zeros((N, T))
    pa[:, idx] = p
    pb = np.zeros((N, T))
    pb[:, idx2] = p
    y = z + pa + pb
    return y

@@ -1,0 +1,173 @@
+from contextlib import ExitStack
+
+import concourse.mybir as mybir
+from concourse.masks import make_identity
+
+K, T, J, N = 512, 2048, 512, 256
+FLOPS = 2 * K * N * (T + J)
+
+F32 = mybir.dt.float32
+BF16 = mybir.dt.bfloat16
+I32 = mybir.dt.int32
+U32 = mybir.dt.uint32
+U16 = mybir.dt.uint16
+U8 = mybir.dt.uint8
+FP8X4 = mybir.dt.float8_e4m3fn_x4
+FP4X4 = mybir.dt.float4_e2m1fn_x4
+MULT = mybir.AluOpType.mult
+ADD = mybir.AluOpType.add
+COPY = mybir.ActivationFunctionType.Copy
+
+P = 128
+PACK = 4
+BANK = 512
+CHUNKS = T // BANK
+BLOCKS = BANK // P
+PART = J // 2
+LIST_COLS = J // 16
+
+
+def load_scales(nc, plane, rows):
+    for q in range(4):
+        nc.sync.dma_start(out=plane[32 * q : 32 * q + 4, :].bitcast(I32), in_=rows[0, 4 * q : 4 * q + 4, :].bitcast(I32))
+
+
+def tile_list_merge_then_spread_kernel(tc, xq_words, xq_scales, wb_words, wb_scales, xf, sh, wm_words, wm_scales, offs, offs2, out):
+    nc = tc.nc
+    with ExitStack() as ctx:
+        lists = ctx.enter_context(tc.tile_pool(name="lists", bufs=1))
+        keep = ctx.enter_context(tc.tile_pool(name="keep", bufs=1))
+        psum = ctx.enter_context(tc.psum_pool(name="psum", bufs=1))
+        banks = [psum.tile([P, BANK], F32, name=f"bank{b}") for b in range(8)]
+
+        ident = keep.tile([P, P], F32)
+        make_identity(nc, ident[:])
+
+        sh_cols = keep.tile([P, PACK], F32)
+        nc.sync.dma_start(out=sh_cols[:], in_=sh.rearrange("o (p c) -> (o p) c", c=PACK))
+        rows = xf.rearrange("(p t) c -> p t c", t=PACK)
+        planes = [keep.tile([P, T], F32, name=f"plane{t}") for t in range(PACK)]
+        first = lists.tile([P, LIST_COLS], U16)
+        second = lists.tile([P, LIST_COLS], U16)
+        nc.sync.dma_start(out=planes[0][:], in_=rows[:, 0, :])
+        nc.sync.dma_start(first[:], offs)
+        nc.sync.dma_start(second[:], offs2)
+        for t in range(1, PACK):
+            nc.sync.dma_start(out=planes[t][:], in_=rows[:, t, :])
+
+        wm_codes = keep.tile([P, 2 * N], U8, align_bytes=64)
+        wm_plane = keep.tile([P, N], U8, align_bytes=64)
+        wb_codes = keep.tile([P, N], U32, align_bytes=64)
+        wb_plane = keep.tile([P, N], U8, align_bytes=64)
+        xq_codes = keep.tile([P, 2 * T], U8, align_bytes=64)
+        xq_plane = keep.tile([P, T], U8, align_bytes=64)
+        for plane in (wm_plane, xq_plane, wb_plane):
+            nc.vector.memset(plane[:].bitcast(I32), 0)
+        nc.sync.dma_start(out=wm_codes[:].bitcast(I32), in_=wm_words[0].bitcast(I32))
+        load_scales(nc, wm_plane, wm_scales)
+        nc.sync.dma_start(out=xq_codes[:].bitcast(I32), in_=xq_words[0].bitcast(I32))
+        nc.sync.dma_start(out=wb_codes[:].bitcast(I32), in_=wb_words[0].rearrange("p n t -> p (n t)").bitcast(I32))
+        load_scales(nc, xq_plane, xq_scales)
+        load_scales(nc, wb_plane, wb_scales)
+
+        pa = [keep.tile([P, T], F32, name=f"pa{h}") for h in range(2)]
+        pb = [keep.tile([P, T], F32, name=f"pb{h}") for h in range(2)]
+        for h in range(2):
+            nc.gpsimd.memset(pa[h][:], 0.0)
+            nc.gpsimd.memset(pb[h][:], 0.0)
+
+        share = keep.tile([P, J], F32)
+        rest = keep.tile([P, J], F32)
+        for c in range(PACK):
+            nc.tensor.transpose(banks[4][:, c * P : (c + 1) * P], sh_cols[:, c : c + 1].to_broadcast([P, P]), ident[:])
+        spread = banks[4][:].rearrange("p (c n) -> p n c", c=PACK)
+        nc.vector.tensor_copy(out=share[:].rearrange("p (n c) -> p n c", c=PACK), in_=spread)
+        nc.scalar.activation(out=rest[:].rearrange("p (n c) -> p n c", c=PACK), in_=spread, func=COPY, scale=-1.0, bias=1.0)
+
+        ma = keep.tile([P, PACK * J], F32)
+        mb = keep.tile([P, PACK * J], F32)
+        for t in range(PACK - 1):
+            cols = slice(t * J, (t + 1) * J)
+            nc.vector.tensor_tensor(ma[:, cols], planes[t][:].indirect(first[:]), share[:], MULT)
+            nc.vector.tensor_tensor(mb[:, cols], planes[t][:].indirect(second[:]), rest[:], MULT)
+
+        p_rows = [keep.tile([P, J], F32, name=f"p{h}") for h in range(2)]
+        t = PACK - 1
+        grouped = keep.tile([P, PART * PACK], BF16, align_bytes=64)
+        for part in range(2):
+            slots = slice(part * PART, (part + 1) * PART)
+            lcols = slice(part * PART // 16, (part + 1) * PART // 16)
+            cols = slice(t * J + part * PART, t * J + (part + 1) * PART)
+            nc.vector.tensor_tensor(ma[:, cols], planes[t][:].indirect(first[:, lcols]), share[:, slots], MULT)
+            nc.vector.tensor_tensor(mb[:, cols], planes[t][:].indirect(second[:, lcols]), rest[:, slots], MULT)
+            va = ma[:].rearrange("p (t j e) -> p j t e", t=PACK, e=2)[:, part * PART // 2 : (part + 1) * PART // 2]
+            vb = mb[:].rearrange("p (t j e) -> p j t e", t=PACK, e=2)[:, part * PART // 2 : (part + 1) * PART // 2]
+            nc.vector.tensor_tensor(grouped[:].rearrange("p (j e t) -> p j t e", t=PACK, e=2), va, vb, ADD)
+            codes = keep.tile([P, PART], U32, align_bytes=64, name=f"codes{part}")
+            scales = keep.tile([P, PART], U8, align_bytes=64, name=f"scales{part}")
+            nc.vector.quantize_mx(out=codes[:].bitcast(FP8X4), scales=scales[:], in_=grouped[:])
+            for h in range(2):
+                bank = banks[4 + 2 * part + h]
+                nc.tensor.matmul_mx(
+                    out=bank[:, 0:PART],
+                    lhsT=wm_codes[:, 2 * P * h : 2 * P * (h + 1)].bitcast(FP4X4),
+                    lhsT_scale=wm_plane[:, P * h : P * (h + 1)],
+                    rhs=codes[:].bitcast(FP8X4),
+                    rhs_scale=scales[:],
+                    start=True,
+                    stop=True,
+                )
+                nc.scalar.copy(out=p_rows[h][:, slots], in_=bank[:, 0:PART])
+
+        def base(h, c, bank):
+            nc.tensor.matmul_mx(
+                out=bank[:],
+                lhsT=wb_codes[:, P * h : P * (h + 1)].bitcast(FP8X4),
+                lhsT_scale=wb_plane[:, P * h : P * (h + 1)],
+                rhs=xq_codes[:, 2 * BANK * c : 2 * BANK * (c + 1)].bitcast(FP4X4),
+                rhs_scale=xq_plane[:, BANK * c : BANK * (c + 1)],
+                start=True,
+                stop=True,
+            )
+
+        z0 = keep.tile([P, T], F32)
+        for c in range(CHUNKS):
+            base(0, c, banks[c])
+            nc.scalar.copy(out=z0[:, c * BANK : (c + 1) * BANK], in_=banks[c][:])
+        for part in range(2):
+            slots = slice(part * PART, (part + 1) * PART)
+            lcols = slice(part * PART // 16, (part + 1) * PART // 16)
+            nc.vector.tensor_copy(pa[0][:].indirect(first[:, lcols]), p_rows[0][:, slots])
+            nc.vector.tensor_copy(pb[0][:].indirect(second[:, lcols]), p_rows[0][:, slots])
+        nc.vector.tensor_copy(pa[1][:].indirect(first[:]), p_rows[1][:])
+        nc.vector.tensor_copy(pb[1][:].indirect(second[:]), p_rows[1][:])
+
+        terms = (z0, pa[0], pb[0])
+        for i, term in enumerate(terms):
+            for c in range(CHUNKS):
+                for b in range(BLOCKS):
+                    nc.tensor.matmul(
+                        banks[c][:, b * P : (b + 1) * P],
+                        lhsT=term[:, c * BANK + b * P : c * BANK + (b + 1) * P],
+                        rhs=ident[:],
+                        is_transpose=True,
+                        start=(i == 0 and b == 0),
+                        stop=(i == len(terms) - 1 and b == BLOCKS - 1),
+                    )
+        for c in range(CHUNKS):
+            turned = keep.tile([P, BANK], F32, name=f"turned{c}")
+            nc.scalar.copy(out=turned[:], in_=banks[c][:])
+            for b in range(BLOCKS):
+                nc.tensor.transpose(banks[4 + c][:, b * P : (b + 1) * P], turned[:, b * P : (b + 1) * P], ident[:])
+            result = keep.tile([P, BANK], F32, name=f"result0_{c}")
+            nc.scalar.copy(out=result[:], in_=banks[4 + c][:])
+            nc.sync.dma_start(out=out[0:P, c * BANK : (c + 1) * BANK], in_=result[:])
+
+        for c in range(CHUNKS):
+            cols = slice(c * BANK, (c + 1) * BANK)
+            base(1, c, banks[c])
+            partial = keep.tile([P, BANK], F32, name=f"partial{c}")
+            nc.vector.tensor_tensor(partial[:], banks[c][:], pa[1][:, cols], ADD)
+            result = keep.tile([P, BANK], F32, name=f"result1_{c}")
+            nc.vector.tensor_tensor(result[:], partial[:], pb[1][:, cols], ADD)
+            nc.sync.dma_start(out=out[P : 2 * P, cols], in_=result[:])

@@ -61,8 +61,9 @@ def tile_list_merge_then_spread_kernel(tc, xq_words, xq_scales, wb_words, wb_sca
         wb_plane = keep.tile([P, N], U8, align_bytes=64)
         xq_codes = keep.tile([P, 2 * T], U8, align_bytes=64)
         xq_plane = keep.tile([P, T], U8, align_bytes=64)
-        for plane in (wm_plane, xq_plane, wb_plane):
-            nc.vector.memset(plane[:].bitcast(I32), 0)
+        nc.gpsimd.memset(wm_plane[:].bitcast(I32), 0)
+        nc.gpsimd.memset(wb_plane[:].bitcast(I32), 0)
+        nc.vector.memset(xq_plane[:].bitcast(I32), 0)
         nc.sync.dma_start(out=wm_codes[:].bitcast(I32), in_=wm_words[0].bitcast(I32))
         load_scales(nc, wm_plane, wm_scales)
         nc.sync.dma_start(out=xq_codes[:].bitcast(I32), in_=xq_words[0].bitcast(I32))
@@ -79,8 +80,8 @@ def tile_list_merge_then_spread_kernel(tc, xq_words, xq_scales, wb_words, wb_sca
         share = keep.tile([P, J], F32)
         rest = keep.tile([P, J], F32)
         for c in range(PACK):
-            nc.tensor.transpose(banks[4][:, c * P : (c + 1) * P], sh_cols[:, c : c + 1].to_broadcast([P, P]), ident[:])
-        spread = banks[4][:].rearrange("p (c n) -> p n c", c=PACK)
+            nc.tensor.transpose(banks[7][:, c * P : (c + 1) * P], sh_cols[:, c : c + 1].to_broadcast([P, P]), ident[:])
+        spread = banks[7][:].rearrange("p (c n) -> p n c", c=PACK)
         nc.vector.tensor_copy(out=share[:].rearrange("p (n c) -> p n c", c=PACK), in_=spread)
         nc.scalar.activation(out=rest[:].rearrange("p (n c) -> p n c", c=PACK), in_=spread, func=COPY, scale=-1.0, bias=1.0)
 
@@ -91,25 +92,30 @@ def tile_list_merge_then_spread_kernel(tc, xq_words, xq_scales, wb_words, wb_sca
             nc.vector.tensor_tensor(ma[:, cols], planes[t][:].indirect(first[:]), share[:], MULT)
             nc.vector.tensor_tensor(mb[:, cols], planes[t][:].indirect(second[:]), rest[:], MULT)
 
-        p_rows = [keep.tile([P, J], F32, name=f"p{h}") for h in range(2)]
+        p0_parts = [keep.tile([P, PART], F32, name=f"p0_{part}") for part in range(2)]
+        p1 = keep.tile([P, J], F32)
         t = PACK - 1
-        grouped = keep.tile([P, PART * PACK], BF16, align_bytes=64)
-        for part in range(2):
+
+        def gather_last(part, m, offsets, weight):
             slots = slice(part * PART, (part + 1) * PART)
             lcols = slice(part * PART // 16, (part + 1) * PART // 16)
             cols = slice(t * J + part * PART, t * J + (part + 1) * PART)
-            nc.vector.tensor_tensor(ma[:, cols], planes[t][:].indirect(first[:, lcols]), share[:, slots], MULT)
-            nc.vector.tensor_tensor(mb[:, cols], planes[t][:].indirect(second[:, lcols]), rest[:, slots], MULT)
-            va = ma[:].rearrange("p (t j e) -> p j t e", t=PACK, e=2)[:, part * PART // 2 : (part + 1) * PART // 2]
-            vb = mb[:].rearrange("p (t j e) -> p j t e", t=PACK, e=2)[:, part * PART // 2 : (part + 1) * PART // 2]
+            nc.vector.tensor_tensor(m[:, cols], planes[t][:].indirect(offsets[:, lcols]), weight[:, slots], MULT)
+
+        def merge(j0, width):
+            grouped = keep.tile([P, width * PACK], BF16, align_bytes=64, name=f"grouped{j0}")
+            va = ma[:].rearrange("p (t j e) -> p j t e", t=PACK, e=2)[:, j0 // 2 : (j0 + width) // 2]
+            vb = mb[:].rearrange("p (t j e) -> p j t e", t=PACK, e=2)[:, j0 // 2 : (j0 + width) // 2]
             nc.vector.tensor_tensor(grouped[:].rearrange("p (j e t) -> p j t e", t=PACK, e=2), va, vb, ADD)
-            codes = keep.tile([P, PART], U32, align_bytes=64, name=f"codes{part}")
-            scales = keep.tile([P, PART], U8, align_bytes=64, name=f"scales{part}")
+            return grouped
+
+        def product(grouped, j0, width, pair):
+            codes = keep.tile([P, width], U32, align_bytes=64, name=f"codes{j0}")
+            scales = keep.tile([P, width], U8, align_bytes=64, name=f"scales{j0}")
             nc.vector.quantize_mx(out=codes[:].bitcast(FP8X4), scales=scales[:], in_=grouped[:])
             for h in range(2):
-                bank = banks[4 + 2 * part + h]
                 nc.tensor.matmul_mx(
-                    out=bank[:, 0:PART],
+                    out=pair[h][:, 0:width],
                     lhsT=wm_codes[:, 2 * P * h : 2 * P * (h + 1)].bitcast(FP4X4),
                     lhsT_scale=wm_plane[:, P * h : P * (h + 1)],
                     rhs=codes[:].bitcast(FP8X4),
@@ -117,7 +123,18 @@ def tile_list_merge_then_spread_kernel(tc, xq_words, xq_scales, wb_words, wb_sca
                     start=True,
                     stop=True,
                 )
-                nc.scalar.copy(out=p_rows[h][:, slots], in_=bank[:, 0:PART])
+                target = p0_parts[j0 // PART][:, j0 % PART : j0 % PART + width] if h == 0 else p1[:, j0 : j0 + width]
+                nc.scalar.copy(out=target, in_=pair[h][:, 0:width])
+
+        gather_last(0, ma, first, share)
+        gather_last(0, mb, second, rest)
+        gather_last(1, ma, first, share)
+        early = merge(0, PART)
+        gather_last(1, mb, second, rest)
+        product(early, 0, PART, banks[4:6])
+        late = [merge(PART + i * P, P) for i in range(2)]
+        for i in range(2):
+            product(late[i], PART + i * P, P, banks[2 * i : 2 * i + 2])
 
         def base(h, c, bank):
             nc.tensor.matmul_mx(
@@ -134,40 +151,52 @@ def tile_list_merge_then_spread_kernel(tc, xq_words, xq_scales, wb_words, wb_sca
         for c in range(CHUNKS):
             base(0, c, banks[c])
             nc.scalar.copy(out=z0[:, c * BANK : (c + 1) * BANK], in_=banks[c][:])
+        z1 = keep.tile([P, T - BANK], F32)
+        for c in range(CHUNKS - 1):
+            base(1, c, banks[c])
+            nc.scalar.copy(out=z1[:, c * BANK : (c + 1) * BANK], in_=banks[c][:])
+        base(1, CHUNKS - 1, banks[6])
         for part in range(2):
-            slots = slice(part * PART, (part + 1) * PART)
             lcols = slice(part * PART // 16, (part + 1) * PART // 16)
-            nc.vector.tensor_copy(pa[0][:].indirect(first[:, lcols]), p_rows[0][:, slots])
-            nc.vector.tensor_copy(pb[0][:].indirect(second[:, lcols]), p_rows[0][:, slots])
-        nc.vector.tensor_copy(pa[1][:].indirect(first[:]), p_rows[1][:])
-        nc.vector.tensor_copy(pb[1][:].indirect(second[:]), p_rows[1][:])
+            nc.vector.tensor_copy(pa[0][:].indirect(first[:, lcols]), p0_parts[part][:])
+            nc.vector.tensor_copy(pb[0][:].indirect(second[:, lcols]), p0_parts[part][:])
+        nc.vector.tensor_copy(pa[1][:].indirect(first[:]), p1[:])
+        nc.vector.tensor_copy(pb[1][:].indirect(second[:]), p1[:])
 
-        terms = (z0, pa[0], pb[0])
-        for i, term in enumerate(terms):
-            for c in range(CHUNKS):
-                for b in range(BLOCKS):
-                    nc.tensor.matmul(
-                        banks[c][:, b * P : (b + 1) * P],
-                        lhsT=term[:, c * BANK + b * P : c * BANK + (b + 1) * P],
-                        rhs=ident[:],
-                        is_transpose=True,
-                        start=(i == 0 and b == 0),
-                        stop=(i == len(terms) - 1 and b == BLOCKS - 1),
-                    )
-        for c in range(CHUNKS):
-            turned = keep.tile([P, BANK], F32, name=f"turned{c}")
-            nc.scalar.copy(out=turned[:], in_=banks[c][:])
+        def turn(c, term, start, stop):
             for b in range(BLOCKS):
-                nc.tensor.transpose(banks[4 + c][:, b * P : (b + 1) * P], turned[:, b * P : (b + 1) * P], ident[:])
-            result = keep.tile([P, BANK], F32, name=f"result0_{c}")
-            nc.scalar.copy(out=result[:], in_=banks[4 + c][:])
-            nc.sync.dma_start(out=out[0:P, c * BANK : (c + 1) * BANK], in_=result[:])
+                nc.tensor.matmul(
+                    banks[c][:, b * P : (b + 1) * P],
+                    lhsT=term[:, b * P : (b + 1) * P],
+                    rhs=ident[:],
+                    is_transpose=True,
+                    start=(start and b == 0),
+                    stop=(stop and b == BLOCKS - 1),
+                )
 
+        for c in range(CHUNKS):
+            turn(c, pb[0][:, c * BANK : (c + 1) * BANK], True, False)
         for c in range(CHUNKS):
             cols = slice(c * BANK, (c + 1) * BANK)
-            base(1, c, banks[c])
-            partial = keep.tile([P, BANK], F32, name=f"partial{c}")
-            nc.vector.tensor_tensor(partial[:], banks[c][:], pa[1][:, cols], ADD)
+            partial0 = keep.tile([P, BANK], F32, name=f"partial0_{c}")
+            nc.gpsimd.tensor_tensor(partial0[:], z0[:, cols], pa[0][:, cols], ADD)
+            turn(c, partial0[:], False, True)
+            turned = keep.tile([P, BANK], F32, name=f"turned{c}")
+            nc.scalar.copy(out=turned[:], in_=banks[c][:])
+            back = banks[(7, 4, 5)[c % 3]]
+            for b in range(BLOCKS):
+                nc.tensor.transpose(back[:, b * P : (b + 1) * P], turned[:, b * P : (b + 1) * P], ident[:])
+            result = keep.tile([P, BANK], F32, name=f"result0_{c}")
+            nc.scalar.copy(out=result[:], in_=back[:])
+            nc.scalar.dma_start(out=out[0:P, cols], in_=result[:])
+
+        partial1 = [keep.tile([P, BANK], F32, name=f"partial1_{c}") for c in range(CHUNKS)]
+        for c in range(CHUNKS - 1):
+            cols = slice(c * BANK, (c + 1) * BANK)
+            nc.gpsimd.tensor_tensor(partial1[c][:], z1[:, cols], pa[1][:, cols], ADD)
+        nc.vector.tensor_tensor(partial1[CHUNKS - 1][:], banks[6][:], pa[1][:, T - BANK : T], ADD)
+        for c in range(CHUNKS):
+            cols = slice(c * BANK, (c + 1) * BANK)
             result = keep.tile([P, BANK], F32, name=f"result1_{c}")
-            nc.vector.tensor_tensor(result[:], partial[:], pb[1][:, cols], ADD)
+            nc.vector.tensor_tensor(result[:], partial1[c][:], pb[1][:, cols], ADD)
             nc.sync.dma_start(out=out[P : 2 * P, cols], in_=result[:])

@@ -25,6 +25,7 @@ CHUNKS = T // BANK
 BLOCKS = BANK // P
 PART = J // 2
 LIST_COLS = J // 16
+SPLIT = CHUNKS // 2
 
 
 def load_scales(nc, plane, rows):
@@ -41,7 +42,8 @@ def tile_list_merge_then_spread_kernel(tc, xq_words, xq_scales, wb_words, wb_sca
         banks = [psum.tile([P, BANK], F32, name=f"bank{b}") for b in range(8)]
 
         ident = keep.tile([P, P], F32)
-        make_identity(nc, ident[:])
+        nc.vector.memset(ident[:], 0.0)
+        make_identity(nc, ident[:], nomemset=True)
 
         sh_cols = keep.tile([P, PACK], F32)
         nc.sync.dma_start(out=sh_cols[:], in_=sh.rearrange("o (p c) -> (o p) c", c=PACK))
@@ -61,21 +63,20 @@ def tile_list_merge_then_spread_kernel(tc, xq_words, xq_scales, wb_words, wb_sca
         wb_plane = keep.tile([P, N], U8, align_bytes=64)
         xq_codes = keep.tile([P, 2 * T], U8, align_bytes=64)
         xq_plane = keep.tile([P, T], U8, align_bytes=64)
-        nc.gpsimd.memset(wm_plane[:].bitcast(I32), 0)
-        nc.gpsimd.memset(wb_plane[:].bitcast(I32), 0)
+        nc.vector.memset(wm_plane[:].bitcast(I32), 0)
+        nc.vector.memset(wb_plane[:].bitcast(I32), 0)
         nc.vector.memset(xq_plane[:].bitcast(I32), 0)
-        nc.sync.dma_start(out=wm_codes[:].bitcast(I32), in_=wm_words[0].bitcast(I32))
-        load_scales(nc, wm_plane, wm_scales)
         nc.sync.dma_start(out=xq_codes[:].bitcast(I32), in_=xq_words[0].bitcast(I32))
         nc.sync.dma_start(out=wb_codes[:].bitcast(I32), in_=wb_words[0].rearrange("p n t -> p (n t)").bitcast(I32))
         load_scales(nc, xq_plane, xq_scales)
         load_scales(nc, wb_plane, wb_scales)
+        nc.sync.dma_start(out=wm_codes[:].bitcast(I32), in_=wm_words[0].bitcast(I32))
+        load_scales(nc, wm_plane, wm_scales)
 
-        pa = [keep.tile([P, T], F32, name=f"pa{h}") for h in range(2)]
-        pb = [keep.tile([P, T], F32, name=f"pb{h}") for h in range(2)]
-        for h in range(2):
-            nc.gpsimd.memset(pa[h][:], 0.0)
-            nc.gpsimd.memset(pb[h][:], 0.0)
+        pa0 = keep.tile([P, T], F32)
+        pb0 = keep.tile([P, T], F32)
+        nc.vector.memset(pa0[:], 0.0)
+        nc.vector.memset(pb0[:], 0.0)
 
         share = keep.tile([P, J], F32)
         rest = keep.tile([P, J], F32)
@@ -84,6 +85,35 @@ def tile_list_merge_then_spread_kernel(tc, xq_words, xq_scales, wb_words, wb_sca
         spread = banks[7][:].rearrange("p (c n) -> p n c", c=PACK)
         nc.vector.tensor_copy(out=share[:].rearrange("p (n c) -> p n c", c=PACK), in_=spread)
         nc.scalar.activation(out=rest[:].rearrange("p (n c) -> p n c", c=PACK), in_=spread, func=COPY, scale=-1.0, bias=1.0)
+
+        def turn(bank, term, start, stop):
+            for b in range(BLOCKS):
+                nc.tensor.matmul(
+                    bank[:, b * P : (b + 1) * P],
+                    lhsT=term[:, b * P : (b + 1) * P],
+                    rhs=ident[:],
+                    is_transpose=True,
+                    start=(start and b == 0),
+                    stop=(stop and b == BLOCKS - 1),
+                )
+
+        def base(h, c, bank):
+            nc.tensor.matmul_mx(
+                out=bank[:],
+                lhsT=wb_codes[:, P * h : P * (h + 1)].bitcast(FP8X4),
+                lhsT_scale=wb_plane[:, P * h : P * (h + 1)],
+                rhs=xq_codes[:, 2 * BANK * c : 2 * BANK * (c + 1)].bitcast(FP4X4),
+                rhs_scale=xq_plane[:, BANK * c : BANK * (c + 1)],
+                start=True,
+                stop=True,
+            )
+
+        z0 = keep.tile([P, T], F32)
+        for c in range(CHUNKS):
+            base(0, c, banks[4 + c])
+            nc.scalar.copy(out=z0[:, c * BANK : (c + 1) * BANK], in_=banks[4 + c][:])
+            if c >= SPLIT:
+                turn(banks[c - SPLIT], z0[:, c * BANK : (c + 1) * BANK], True, False)
 
         ma = keep.tile([P, PACK * J], F32)
         mb = keep.tile([P, PACK * J], F32)
@@ -110,8 +140,8 @@ def tile_list_merge_then_spread_kernel(tc, xq_words, xq_scales, wb_words, wb_sca
             return grouped
 
         def product(grouped, j0, width, pair):
-            codes = keep.tile([P, width], U32, align_bytes=64, name=f"codes{j0}")
-            scales = keep.tile([P, width], U8, align_bytes=64, name=f"scales{j0}")
+            codes = keep.tile([P, width], U32, align_bytes=64, name=f"codes{j0}", tag=f"codes{j0}")
+            scales = keep.tile([P, width], U8, align_bytes=64, name=f"scales{j0}", tag=f"scales{j0}")
             nc.vector.quantize_mx(out=codes[:].bitcast(FP8X4), scales=scales[:], in_=grouped[:])
             for h in range(2):
                 nc.tensor.matmul_mx(
@@ -134,69 +164,63 @@ def tile_list_merge_then_spread_kernel(tc, xq_words, xq_scales, wb_words, wb_sca
         product(early, 0, PART, banks[4:6])
         late = [merge(PART + i * P, P) for i in range(2)]
         for i in range(2):
-            product(late[i], PART + i * P, P, banks[2 * i : 2 * i + 2])
+            product(late[i], PART + i * P, P, banks[6 - 2 * i : 8 - 2 * i])
 
-        def base(h, c, bank):
-            nc.tensor.matmul_mx(
-                out=bank[:],
-                lhsT=wb_codes[:, P * h : P * (h + 1)].bitcast(FP8X4),
-                lhsT_scale=wb_plane[:, P * h : P * (h + 1)],
-                rhs=xq_codes[:, 2 * BANK * c : 2 * BANK * (c + 1)].bitcast(FP4X4),
-                rhs_scale=xq_plane[:, BANK * c : BANK * (c + 1)],
-                start=True,
-                stop=True,
-            )
+        pa1 = keep.tile([P, T], F32, align_bytes=64, tag=f"codes{J - P}")
+        pb1 = keep.tile([P, T], F32, align_bytes=64, tag=f"scales{J - P}")
+        nc.gpsimd.memset(pa1[:], 0.0)
+        nc.gpsimd.memset(pb1[:], 0.0)
 
-        z0 = keep.tile([P, T], F32)
+        z1 = keep.tile([P, T], F32)
         for c in range(CHUNKS):
-            base(0, c, banks[c])
-            nc.scalar.copy(out=z0[:, c * BANK : (c + 1) * BANK], in_=banks[c][:])
-        z1 = keep.tile([P, T - BANK], F32)
-        for c in range(CHUNKS - 1):
-            base(1, c, banks[c])
-            nc.scalar.copy(out=z1[:, c * BANK : (c + 1) * BANK], in_=banks[c][:])
-        base(1, CHUNKS - 1, banks[6])
+            bank = banks[4 + (c + 2) % 4]
+            base(1, c, bank)
+            nc.scalar.copy(out=z1[:, c * BANK : (c + 1) * BANK], in_=bank[:])
+
         for part in range(2):
             lcols = slice(part * PART // 16, (part + 1) * PART // 16)
-            nc.vector.tensor_copy(pa[0][:].indirect(first[:, lcols]), p0_parts[part][:])
-            nc.vector.tensor_copy(pb[0][:].indirect(second[:, lcols]), p0_parts[part][:])
-        nc.vector.tensor_copy(pa[1][:].indirect(first[:]), p1[:])
-        nc.vector.tensor_copy(pb[1][:].indirect(second[:]), p1[:])
+            nc.vector.tensor_copy(pa0[:].indirect(first[:, lcols]), p0_parts[part][:])
+            nc.vector.tensor_copy(pb0[:].indirect(second[:, lcols]), p0_parts[part][:])
+        nc.vector.tensor_copy(pa1[:].indirect(first[:]), p1[:])
+        nc.vector.tensor_copy(pb1[:].indirect(second[:]), p1[:])
 
-        def turn(c, term, start, stop):
-            for b in range(BLOCKS):
-                nc.tensor.matmul(
-                    banks[c][:, b * P : (b + 1) * P],
-                    lhsT=term[:, b * P : (b + 1) * P],
-                    rhs=ident[:],
-                    is_transpose=True,
-                    start=(start and b == 0),
-                    stop=(stop and b == BLOCKS - 1),
-                )
+        def chunk(c):
+            return slice(c * BANK, (c + 1) * BANK)
 
-        for c in range(CHUNKS):
-            turn(c, pb[0][:, c * BANK : (c + 1) * BANK], True, False)
-        for c in range(CHUNKS):
-            cols = slice(c * BANK, (c + 1) * BANK)
-            partial0 = keep.tile([P, BANK], F32, name=f"partial0_{c}")
-            nc.gpsimd.tensor_tensor(partial0[:], z0[:, cols], pa[0][:, cols], ADD)
-            turn(c, partial0[:], False, True)
-            turned = keep.tile([P, BANK], F32, name=f"turned{c}")
-            nc.scalar.copy(out=turned[:], in_=banks[c][:])
-            back = banks[(7, 4, 5)[c % 3]]
-            for b in range(BLOCKS):
-                nc.tensor.transpose(back[:, b * P : (b + 1) * P], turned[:, b * P : (b + 1) * P], ident[:])
+        def turn_back(bank, back, name):
+            turned = keep.tile([P, BANK], F32, name=name)
+            nc.scalar.copy(out=turned[:], in_=bank[:])
+            turn(back, turned[:], True, True)
+
+        for c in range(SPLIT, CHUNKS):
+            turn(banks[c - SPLIT], pa0[:, chunk(c)], False, False)
+        for c in range(SPLIT, CHUNKS):
+            turn(banks[c - SPLIT], pb0[:, chunk(c)], False, True)
+            turn_back(banks[c - SPLIT], banks[c], f"turned0_{c}")
             result = keep.tile([P, BANK], F32, name=f"result0_{c}")
-            nc.scalar.copy(out=result[:], in_=back[:])
-            nc.scalar.dma_start(out=out[0:P, cols], in_=result[:])
+            nc.scalar.copy(out=result[:], in_=banks[c][:])
+            nc.sync.dma_start(out=out[0:P, chunk(c)], in_=result[:])
+        partial0 = keep.tile([P, SPLIT * BANK], F32)
+        for c in range(SPLIT):
+            nc.gpsimd.tensor_tensor(partial0[:, chunk(c)], z0[:, chunk(c)], pa0[:, chunk(c)], ADD)
+        for c in range(SPLIT):
+            result = keep.tile([P, BANK], F32, name=f"result0_{c}")
+            nc.gpsimd.tensor_tensor(result[:], partial0[:, chunk(c)], pb0[:, chunk(c)], ADD)
+            nc.sync.dma_start(out=out[0:P, chunk(c)], in_=result[:])
 
-        partial1 = [keep.tile([P, BANK], F32, name=f"partial1_{c}") for c in range(CHUNKS)]
-        for c in range(CHUNKS - 1):
-            cols = slice(c * BANK, (c + 1) * BANK)
-            nc.gpsimd.tensor_tensor(partial1[c][:], z1[:, cols], pa[1][:, cols], ADD)
-        nc.vector.tensor_tensor(partial1[CHUNKS - 1][:], banks[6][:], pa[1][:, T - BANK : T], ADD)
-        for c in range(CHUNKS):
-            cols = slice(c * BANK, (c + 1) * BANK)
-            result = keep.tile([P, BANK], F32, name=f"result1_{c}")
-            nc.vector.tensor_tensor(result[:], partial1[c][:], pb[1][:, cols], ADD)
-            nc.sync.dma_start(out=out[P : 2 * P, cols], in_=result[:])
+        partial1 = {}
+        for c in range(SPLIT, CHUNKS):
+            turn(banks[c - SPLIT], z1[:, chunk(c)], True, False)
+            turn(banks[c - SPLIT], pa1[:, chunk(c)], False, True)
+            turn_back(banks[c - SPLIT], banks[4 + c], f"turned1_{c}")
+            partial1[c] = banks[4 + c]
+        for c in range(SPLIT):
+            partial1[c] = keep.tile([P, BANK], F32, name=f"partial1_{c}")
+            nc.gpsimd.tensor_tensor(partial1[c][:], z1[:, chunk(c)], pa1[:, chunk(c)], ADD)
+        for i, c in enumerate(list(range(SPLIT, CHUNKS)) + list(range(SPLIT))):
+            width = BANK // 2 if i == 0 else BANK
+            for c0 in range(0, BANK, width):
+                cols = slice(c * BANK + c0, c * BANK + c0 + width)
+                result = keep.tile([P, width], F32, name=f"result1_{c}_{c0}")
+                nc.vector.tensor_tensor(result[:], partial1[c][:, c0 : c0 + width], pb1[:, cols], ADD)
+                nc.scalar.dma_start(out=out[P : 2 * P, cols], in_=result[:])

@@ -28,9 +28,9 @@ LIST_COLS = J // 16
 SPLIT = CHUNKS // 2
 
 
-def load_scales(nc, plane, rows):
+def load_scales(queue, plane, rows):
     for q in range(4):
-        nc.sync.dma_start(out=plane[32 * q : 32 * q + 4, :].bitcast(I32), in_=rows[0, 4 * q : 4 * q + 4, :].bitcast(I32))
+        queue.dma_start(out=plane[32 * q : 32 * q + 4, :].bitcast(I32), in_=rows[0, 4 * q : 4 * q + 4, :].bitcast(I32))
 
 
 def tile_list_merge_then_spread_kernel(tc, xq_words, xq_scales, wb_words, wb_scales, xf, sh, wm_words, wm_scales, offs, offs2, out):
@@ -63,15 +63,15 @@ def tile_list_merge_then_spread_kernel(tc, xq_words, xq_scales, wb_words, wb_sca
         wb_plane = keep.tile([P, N], U8, align_bytes=64)
         xq_codes = keep.tile([P, 2 * T], U8, align_bytes=64)
         xq_plane = keep.tile([P, T], U8, align_bytes=64)
-        nc.vector.memset(wm_plane[:].bitcast(I32), 0)
         nc.vector.memset(wb_plane[:].bitcast(I32), 0)
+        nc.vector.memset(wm_plane[:].bitcast(I32), 0)
         nc.vector.memset(xq_plane[:].bitcast(I32), 0)
         nc.sync.dma_start(out=xq_codes[:].bitcast(I32), in_=xq_words[0].bitcast(I32))
         nc.sync.dma_start(out=wb_codes[:].bitcast(I32), in_=wb_words[0].rearrange("p n t -> p (n t)").bitcast(I32))
-        load_scales(nc, xq_plane, xq_scales)
-        load_scales(nc, wb_plane, wb_scales)
+        load_scales(nc.sync, xq_plane, xq_scales)
+        load_scales(nc.gpsimd, wb_plane, wb_scales)
         nc.sync.dma_start(out=wm_codes[:].bitcast(I32), in_=wm_words[0].bitcast(I32))
-        load_scales(nc, wm_plane, wm_scales)
+        load_scales(nc.sync, wm_plane, wm_scales)
 
         pa0 = keep.tile([P, T], F32)
         pb0 = keep.tile([P, T], F32)
@@ -86,12 +86,12 @@ def tile_list_merge_then_spread_kernel(tc, xq_words, xq_scales, wb_words, wb_sca
         nc.vector.tensor_copy(out=share[:].rearrange("p (n c) -> p n c", c=PACK), in_=spread)
         nc.scalar.activation(out=rest[:].rearrange("p (n c) -> p n c", c=PACK), in_=spread, func=COPY, scale=-1.0, bias=1.0)
 
-        def turn(bank, term, start, stop):
+        def turn(bank, term, start, stop, unit=ident):
             for b in range(BLOCKS):
                 nc.tensor.matmul(
                     bank[:, b * P : (b + 1) * P],
                     lhsT=term[:, b * P : (b + 1) * P],
-                    rhs=ident[:],
+                    rhs=unit[:],
                     is_transpose=True,
                     start=(start and b == 0),
                     stop=(stop and b == BLOCKS - 1),
@@ -108,12 +108,16 @@ def tile_list_merge_then_spread_kernel(tc, xq_words, xq_scales, wb_words, wb_sca
                 stop=True,
             )
 
-        z0 = keep.tile([P, T], F32)
-        for c in range(CHUNKS):
-            base(0, c, banks[4 + c])
-            nc.scalar.copy(out=z0[:, c * BANK : (c + 1) * BANK], in_=banks[4 + c][:])
-            if c >= SPLIT:
-                turn(banks[c - SPLIT], z0[:, c * BANK : (c + 1) * BANK], True, False)
+        def chunk(c):
+            return slice(c * BANK, (c + 1) * BANK)
+
+        z = [keep.tile([P, T], F32, name=f"z{h}") for h in range(2)]
+        for h in range(2):
+            for c in range(SPLIT, CHUNKS):
+                i = h * SPLIT + c - SPLIT
+                base(h, c, banks[4 + i])
+                nc.scalar.copy(out=z[h][:, chunk(c)], in_=banks[4 + i][:])
+                turn(banks[i], z[h][:, chunk(c)], True, False)
 
         ma = keep.tile([P, PACK * J], F32)
         mb = keep.tile([P, PACK * J], F32)
@@ -171,11 +175,11 @@ def tile_list_merge_then_spread_kernel(tc, xq_words, xq_scales, wb_words, wb_sca
         nc.gpsimd.memset(pa1[:], 0.0)
         nc.gpsimd.memset(pb1[:], 0.0)
 
-        z1 = keep.tile([P, T], F32)
-        for c in range(CHUNKS):
-            bank = banks[4 + (c + 2) % 4]
-            base(1, c, bank)
-            nc.scalar.copy(out=z1[:, c * BANK : (c + 1) * BANK], in_=bank[:])
+        for h in range(2):
+            for c in range(SPLIT):
+                bank = banks[6 - 2 * h + c]
+                base(h, c, bank)
+                nc.scalar.copy(out=z[h][:, chunk(c)], in_=bank[:])
 
         for part in range(2):
             lcols = slice(part * PART // 16, (part + 1) * PART // 16)
@@ -184,11 +188,8 @@ def tile_list_merge_then_spread_kernel(tc, xq_words, xq_scales, wb_words, wb_sca
         nc.vector.tensor_copy(pa1[:].indirect(first[:]), p1[:])
         nc.vector.tensor_copy(pb1[:].indirect(second[:]), p1[:])
 
-        def chunk(c):
-            return slice(c * BANK, (c + 1) * BANK)
-
         def turn_back(bank, back, name):
-            turned = keep.tile([P, BANK], F32, name=name)
+            turned = keep.tile([P, BANK], F32, name=name, tag=name)
             nc.scalar.copy(out=turned[:], in_=bank[:])
             turn(back, turned[:], True, True)
 
@@ -196,31 +197,33 @@ def tile_list_merge_then_spread_kernel(tc, xq_words, xq_scales, wb_words, wb_sca
             turn(banks[c - SPLIT], pa0[:, chunk(c)], False, False)
         for c in range(SPLIT, CHUNKS):
             turn(banks[c - SPLIT], pb0[:, chunk(c)], False, True)
-            turn_back(banks[c - SPLIT], banks[c], f"turned0_{c}")
+            turn_back(banks[c - SPLIT], banks[2 + c], f"turned0_{c}")
             result = keep.tile([P, BANK], F32, name=f"result0_{c}")
-            nc.scalar.copy(out=result[:], in_=banks[c][:])
+            nc.scalar.copy(out=result[:], in_=banks[2 + c][:])
             nc.sync.dma_start(out=out[0:P, chunk(c)], in_=result[:])
         partial0 = keep.tile([P, SPLIT * BANK], F32)
         for c in range(SPLIT):
-            nc.gpsimd.tensor_tensor(partial0[:, chunk(c)], z0[:, chunk(c)], pa0[:, chunk(c)], ADD)
+            nc.gpsimd.tensor_tensor(partial0[:, chunk(c)], z[0][:, chunk(c)], pa0[:, chunk(c)], ADD)
         for c in range(SPLIT):
             result = keep.tile([P, BANK], F32, name=f"result0_{c}")
             nc.gpsimd.tensor_tensor(result[:], partial0[:, chunk(c)], pb0[:, chunk(c)], ADD)
             nc.sync.dma_start(out=out[0:P, chunk(c)], in_=result[:])
 
+        late_ident = keep.tile([P, P], F32, tag=f"turned0_{CHUNKS - 1}")
+        nc.scalar.copy(out=late_ident[:], in_=ident[:])
         partial1 = {}
         for c in range(SPLIT, CHUNKS):
-            turn(banks[c - SPLIT], z1[:, chunk(c)], True, False)
-            turn(banks[c - SPLIT], pa1[:, chunk(c)], False, True)
-            turn_back(banks[c - SPLIT], banks[4 + c], f"turned1_{c}")
+            turn(banks[c], pa1[:, chunk(c)], False, True, late_ident)
+            turn_back(banks[c], banks[4 + c], f"turned1_{c}")
             partial1[c] = banks[4 + c]
         for c in range(SPLIT):
-            partial1[c] = keep.tile([P, BANK], F32, name=f"partial1_{c}")
-            nc.gpsimd.tensor_tensor(partial1[c][:], z1[:, chunk(c)], pa1[:, chunk(c)], ADD)
-        for i, c in enumerate(list(range(SPLIT, CHUNKS)) + list(range(SPLIT))):
-            width = BANK // 2 if i == 0 else BANK
+            partial1[c] = keep.tile([P, BANK], F32, name=f"partial1_{c}", tag=f"partial1_{c}")
+            nc.gpsimd.tensor_tensor(partial1[c][:], z[1][:, chunk(c)], pa1[:, chunk(c)], ADD)
+        for c in range(CHUNKS):
+            width = BANK // 2 if c == 0 else BANK
             for c0 in range(0, BANK, width):
                 cols = slice(c * BANK + c0, c * BANK + c0 + width)
-                result = keep.tile([P, width], F32, name=f"result1_{c}_{c0}")
+                tag = f"partial1_{c - SPLIT}" if c >= SPLIT else f"result1_{c}_{c0}"
+                result = keep.tile([P, width], F32, name=f"result1_{c}_{c0}", tag=tag)
                 nc.vector.tensor_tensor(result[:], partial1[c][:, c0 : c0 + width], pb1[:, cols], ADD)
                 nc.scalar.dma_start(out=out[P : 2 * P, cols], in_=result[:])

@@ -61,17 +61,18 @@ def tile_list_merge_then_spread_kernel(tc, xq_words, xq_scales, wb_words, wb_sca
         wm_plane = keep.tile([P, N], U8, align_bytes=64)
         wb_codes = keep.tile([P, N], U32, align_bytes=64)
         wb_plane = keep.tile([P, N], U8, align_bytes=64)
-        xq_codes = keep.tile([P, 2 * T], U8, align_bytes=64)
+        xq_codes = [keep.tile([P, T], U8, align_bytes=64, name=f"xq_codes{i}") for i in range(2)]
         xq_plane = keep.tile([P, T], U8, align_bytes=64)
         nc.vector.memset(wb_plane[:].bitcast(I32), 0)
         nc.vector.memset(wm_plane[:].bitcast(I32), 0)
         nc.vector.memset(xq_plane[:].bitcast(I32), 0)
-        nc.sync.dma_start(out=xq_codes[:].bitcast(I32), in_=xq_words[0].bitcast(I32))
+        nc.sync.dma_start(out=xq_codes[1][:].bitcast(I32), in_=xq_words[0, :, T : 2 * T].bitcast(I32))
         nc.sync.dma_start(out=wb_codes[:].bitcast(I32), in_=wb_words[0].rearrange("p n t -> p (n t)").bitcast(I32))
         load_scales(nc.sync, xq_plane, xq_scales)
         load_scales(nc.gpsimd, wb_plane, wb_scales)
         nc.sync.dma_start(out=wm_codes[:].bitcast(I32), in_=wm_words[0].bitcast(I32))
         load_scales(nc.sync, wm_plane, wm_scales)
+        nc.sync.dma_start(out=xq_codes[0][:].bitcast(I32), in_=xq_words[0, :, 0:T].bitcast(I32))
 
         pa0 = keep.tile([P, T], F32)
         pb0 = keep.tile([P, T], F32)
@@ -102,7 +103,7 @@ def tile_list_merge_then_spread_kernel(tc, xq_words, xq_scales, wb_words, wb_sca
                 out=bank[:],
                 lhsT=wb_codes[:, P * h : P * (h + 1)].bitcast(FP8X4),
                 lhsT_scale=wb_plane[:, P * h : P * (h + 1)],
-                rhs=xq_codes[:, 2 * BANK * c : 2 * BANK * (c + 1)].bitcast(FP4X4),
+                rhs=xq_codes[c // SPLIT][:, 2 * BANK * (c % SPLIT) : 2 * BANK * (c % SPLIT + 1)].bitcast(FP4X4),
                 rhs_scale=xq_plane[:, BANK * c : BANK * (c + 1)],
                 start=True,
                 stop=True,

from contextlib import ExitStack

import concourse.mybir as mybir
from concourse.masks import make_identity

K, T, J, N = 512, 2048, 512, 256
FLOPS = 2 * K * N * (T + J)

F32 = mybir.dt.float32
BF16 = mybir.dt.bfloat16
I32 = mybir.dt.int32
U32 = mybir.dt.uint32
U16 = mybir.dt.uint16
U8 = mybir.dt.uint8
FP8X4 = mybir.dt.float8_e4m3fn_x4
FP4X4 = mybir.dt.float4_e2m1fn_x4
MULT = mybir.AluOpType.mult
ADD = mybir.AluOpType.add
COPY = mybir.ActivationFunctionType.Copy

P = 128
PACK = 4
BANK = 512
CHUNKS = T // BANK
BLOCKS = BANK // P
PART = J // 2
LIST_COLS = J // 16
SPLIT = CHUNKS // 2


def load_scales(queue, plane, rows):
    for q in range(4):
        queue.dma_start(out=plane[32 * q : 32 * q + 4, :].bitcast(I32), in_=rows[0, 4 * q : 4 * q + 4, :].bitcast(I32))


def tile_list_merge_then_spread_kernel(tc, xq_words, xq_scales, wb_words, wb_scales, xf, sh, wm_words, wm_scales, offs, offs2, out):
    nc = tc.nc
    with ExitStack() as ctx:
        lists = ctx.enter_context(tc.tile_pool(name="lists", bufs=1))
        keep = ctx.enter_context(tc.tile_pool(name="keep", bufs=1))
        psum = ctx.enter_context(tc.psum_pool(name="psum", bufs=1))
        banks = [psum.tile([P, BANK], F32, name=f"bank{b}") for b in range(8)]

        ident = keep.tile([P, P], F32)
        nc.vector.memset(ident[:], 0.0)
        make_identity(nc, ident[:], nomemset=True)

        sh_cols = keep.tile([P, PACK], F32)
        nc.sync.dma_start(out=sh_cols[:], in_=sh.rearrange("o (p c) -> (o p) c", c=PACK))
        rows = xf.rearrange("(p t) c -> p t c", t=PACK)
        planes = [keep.tile([P, T], F32, name=f"plane{t}") for t in range(PACK)]
        first = lists.tile([P, LIST_COLS], U16)
        second = lists.tile([P, LIST_COLS], U16)
        nc.sync.dma_start(out=planes[0][:], in_=rows[:, 0, :])
        nc.sync.dma_start(first[:], offs)
        nc.sync.dma_start(second[:], offs2)
        for t in range(1, PACK):
            nc.sync.dma_start(out=planes[t][:], in_=rows[:, t, :])

        wm_codes = keep.tile([P, 2 * N], U8, align_bytes=64)
        wm_plane = keep.tile([P, N], U8, align_bytes=64)
        wb_codes = keep.tile([P, N], U32, align_bytes=64)
        wb_plane = keep.tile([P, N], U8, align_bytes=64)
        xq_codes = [keep.tile([P, T], U8, align_bytes=64, name=f"xq_codes{i}") for i in range(2)]
        xq_plane = keep.tile([P, T], U8, align_bytes=64)
        nc.vector.memset(wb_plane[:].bitcast(I32), 0)
        nc.vector.memset(wm_plane[:].bitcast(I32), 0)
        nc.vector.memset(xq_plane[:].bitcast(I32), 0)
        nc.sync.dma_start(out=xq_codes[1][:].bitcast(I32), in_=xq_words[0, :, T : 2 * T].bitcast(I32))
        nc.sync.dma_start(out=wb_codes[:].bitcast(I32), in_=wb_words[0].rearrange("p n t -> p (n t)").bitcast(I32))
        load_scales(nc.sync, xq_plane, xq_scales)
        load_scales(nc.gpsimd, wb_plane, wb_scales)
        nc.sync.dma_start(out=wm_codes[:].bitcast(I32), in_=wm_words[0].bitcast(I32))
        load_scales(nc.sync, wm_plane, wm_scales)
        nc.sync.dma_start(out=xq_codes[0][:].bitcast(I32), in_=xq_words[0, :, 0:T].bitcast(I32))

        pa0 = keep.tile([P, T], F32)
        pb0 = keep.tile([P, T], F32)
        nc.vector.memset(pa0[:], 0.0)
        nc.vector.memset(pb0[:], 0.0)

        share = keep.tile([P, J], F32)
        rest = keep.tile([P, J], F32)
        for c in range(PACK):
            nc.tensor.transpose(banks[7][:, c * P : (c + 1) * P], sh_cols[:, c : c + 1].to_broadcast([P, P]), ident[:])
        spread = banks[7][:].rearrange("p (c n) -> p n c", c=PACK)
        nc.vector.tensor_copy(out=share[:].rearrange("p (n c) -> p n c", c=PACK), in_=spread)
        nc.scalar.activation(out=rest[:].rearrange("p (n c) -> p n c", c=PACK), in_=spread, func=COPY, scale=-1.0, bias=1.0)

        def turn(bank, term, start, stop, unit=ident):
            for b in range(BLOCKS):
                nc.tensor.matmul(
                    bank[:, b * P : (b + 1) * P],
                    lhsT=term[:, b * P : (b + 1) * P],
                    rhs=unit[:],
                    is_transpose=True,
                    start=(start and b == 0),
                    stop=(stop and b == BLOCKS - 1),
                )

        def base(h, c, bank):
            nc.tensor.matmul_mx(
                out=bank[:],
                lhsT=wb_codes[:, P * h : P * (h + 1)].bitcast(FP8X4),
                lhsT_scale=wb_plane[:, P * h : P * (h + 1)],
                rhs=xq_codes[c // SPLIT][:, 2 * BANK * (c % SPLIT) : 2 * BANK * (c % SPLIT + 1)].bitcast(FP4X4),
                rhs_scale=xq_plane[:, BANK * c : BANK * (c + 1)],
                start=True,
                stop=True,
            )

        def chunk(c):
            return slice(c * BANK, (c + 1) * BANK)

        z = [keep.tile([P, T], F32, name=f"z{h}") for h in range(2)]
        for h in range(2):
            for c in range(SPLIT, CHUNKS):
                i = h * SPLIT + c - SPLIT
                base(h, c, banks[4 + i])
                nc.scalar.copy(out=z[h][:, chunk(c)], in_=banks[4 + i][:])
                turn(banks[i], z[h][:, chunk(c)], True, False)

        ma = keep.tile([P, PACK * J], F32)
        mb = keep.tile([P, PACK * J], F32)
        for t in range(PACK - 1):
            cols = slice(t * J, (t + 1) * J)
            nc.vector.tensor_tensor(ma[:, cols], planes[t][:].indirect(first[:]), share[:], MULT)
            nc.vector.tensor_tensor(mb[:, cols], planes[t][:].indirect(second[:]), rest[:], MULT)

        p0_parts = [keep.tile([P, PART], F32, name=f"p0_{part}") for part in range(2)]
        p1 = keep.tile([P, J], F32)
        t = PACK - 1

        def gather_last(part, m, offsets, weight):
            slots = slice(part * PART, (part + 1) * PART)
            lcols = slice(part * PART // 16, (part + 1) * PART // 16)
            cols = slice(t * J + part * PART, t * J + (part + 1) * PART)
            nc.vector.tensor_tensor(m[:, cols], planes[t][:].indirect(offsets[:, lcols]), weight[:, slots], MULT)

        def merge(j0, width):
            grouped = keep.tile([P, width * PACK], BF16, align_bytes=64, name=f"grouped{j0}")
            va = ma[:].rearrange("p (t j e) -> p j t e", t=PACK, e=2)[:, j0 // 2 : (j0 + width) // 2]
            vb = mb[:].rearrange("p (t j e) -> p j t e", t=PACK, e=2)[:, j0 // 2 : (j0 + width) // 2]
            nc.vector.tensor_tensor(grouped[:].rearrange("p (j e t) -> p j t e", t=PACK, e=2), va, vb, ADD)
            return grouped

        def product(grouped, j0, width, pair):
            codes = keep.tile([P, width], U32, align_bytes=64, name=f"codes{j0}", tag=f"codes{j0}")
            scales = keep.tile([P, width], U8, align_bytes=64, name=f"scales{j0}", tag=f"scales{j0}")
            nc.vector.quantize_mx(out=codes[:].bitcast(FP8X4), scales=scales[:], in_=grouped[:])
            for h in range(2):
                nc.tensor.matmul_mx(
                    out=pair[h][:, 0:width],
                    lhsT=wm_codes[:, 2 * P * h : 2 * P * (h + 1)].bitcast(FP4X4),
                    lhsT_scale=wm_plane[:, P * h : P * (h + 1)],
                    rhs=codes[:].bitcast(FP8X4),
                    rhs_scale=scales[:],
                    start=True,
                    stop=True,
                )
                target = p0_parts[j0 // PART][:, j0 % PART : j0 % PART + width] if h == 0 else p1[:, j0 : j0 + width]
                nc.scalar.copy(out=target, in_=pair[h][:, 0:width])

        gather_last(0, ma, first, share)
        gather_last(0, mb, second, rest)
        gather_last(1, ma, first, share)
        early = merge(0, PART)
        gather_last(1, mb, second, rest)
        product(early, 0, PART, banks[4:6])
        late = [merge(PART + i * P, P) for i in range(2)]
        for i in range(2):
            product(late[i], PART + i * P, P, banks[6 - 2 * i : 8 - 2 * i])

        pa1 = keep.tile([P, T], F32, align_bytes=64, tag=f"codes{J - P}")
        pb1 = keep.tile([P, T], F32, align_bytes=64, tag=f"scales{J - P}")
        nc.gpsimd.memset(pa1[:], 0.0)
        nc.gpsimd.memset(pb1[:], 0.0)

        for h in range(2):
            for c in range(SPLIT):
                bank = banks[6 - 2 * h + c]
                base(h, c, bank)
                nc.scalar.copy(out=z[h][:, chunk(c)], in_=bank[:])

        for part in range(2):
            lcols = slice(part * PART // 16, (part + 1) * PART // 16)
            nc.vector.tensor_copy(pa0[:].indirect(first[:, lcols]), p0_parts[part][:])
            nc.vector.tensor_copy(pb0[:].indirect(second[:, lcols]), p0_parts[part][:])
        nc.vector.tensor_copy(pa1[:].indirect(first[:]), p1[:])
        nc.vector.tensor_copy(pb1[:].indirect(second[:]), p1[:])

        def turn_back(bank, back, name):
            turned = keep.tile([P, BANK], F32, name=name, tag=name)
            nc.scalar.copy(out=turned[:], in_=bank[:])
            turn(back, turned[:], True, True)

        for c in range(SPLIT, CHUNKS):
            turn(banks[c - SPLIT], pa0[:, chunk(c)], False, False)
        for c in range(SPLIT, CHUNKS):
            turn(banks[c - SPLIT], pb0[:, chunk(c)], False, True)
            turn_back(banks[c - SPLIT], banks[2 + c], f"turned0_{c}")
            result = keep.tile([P, BANK], F32, name=f"result0_{c}")
            nc.scalar.copy(out=result[:], in_=banks[2 + c][:])
            nc.sync.dma_start(out=out[0:P, chunk(c)], in_=result[:])
        partial0 = keep.tile([P, SPLIT * BANK], F32)
        for c in range(SPLIT):
            nc.gpsimd.tensor_tensor(partial0[:, chunk(c)], z[0][:, chunk(c)], pa0[:, chunk(c)], ADD)
        for c in range(SPLIT):
            result = keep.tile([P, BANK], F32, name=f"result0_{c}")
            nc.gpsimd.tensor_tensor(result[:], partial0[:, chunk(c)], pb0[:, chunk(c)], ADD)
            nc.sync.dma_start(out=out[0:P, chunk(c)], in_=result[:])

        late_ident = keep.tile([P, P], F32, tag=f"turned0_{CHUNKS - 1}")
        nc.scalar.copy(out=late_ident[:], in_=ident[:])
        partial1 = {}
        for c in range(SPLIT, CHUNKS):
            turn(banks[c], pa1[:, chunk(c)], False, True, late_ident)
            turn_back(banks[c], banks[4 + c], f"turned1_{c}")
            partial1[c] = banks[4 + c]
        for c in range(SPLIT):
            partial1[c] = keep.tile([P, BANK], F32, name=f"partial1_{c}", tag=f"partial1_{c}")
            nc.gpsimd.tensor_tensor(partial1[c][:], z[1][:, chunk(c)], pa1[:, chunk(c)], ADD)
        for c in range(CHUNKS):
            width = BANK // 2 if c == 0 else BANK
            for c0 in range(0, BANK, width):
                cols = slice(c * BANK + c0, c * BANK + c0 + width)
                tag = f"partial1_{c - SPLIT}" if c >= SPLIT else f"result1_{c}_{c0}"
                result = keep.tile([P, width], F32, name=f"result1_{c}_{c0}", tag=tag)
                nc.vector.tensor_tensor(result[:], partial1[c][:, c0 : c0 + width], pb1[:, cols], ADD)
                nc.scalar.dma_start(out=out[P : 2 * P, cols], in_=result[:])
